import numpy as np
CORES = [7,6,5,4,3,2,1,0]
N = 8
ROOT = 0
def setup_inputs(rng):
    return {"x": rng.standard_normal((N, 128, 512), dtype=np.float32)}
def reference(x):
    return {"y": np.broadcast_to(x[ROOT], x.shape)}

@@ -1,0 +1,42 @@
+import concourse.bass as bass
+
+SCRATCH = {
+    "land": ("sbuf", [128, 512], "float32"),
+}
+SEMAPHORES = ["loaded", "read", "arrived", "stored"]
+
+ENGINES = 16
+
+
+def rank_program(g, core, T, topo):
+    rank = T.rank_of(core)
+    if rank is None:
+        return
+    root = T.cores[0]
+
+    if core == root:
+        g.dma_start(T.land[:], T.x[:]).then_inc(T.sem.loaded, 16)
+        g.wait_ge(T.sem.loaded, 16)
+        others = [c for c in T.cores if c != root]
+        ids = []
+        for c in others:
+            a = topo.addr(c)
+            ids.append(bass.DstId(rid=a[0], pnc=a[1]))
+        g.remote_dma_fused(
+            [bass.RemoteDMATransfer(
+                dst_ids=ids,
+                dma_engine_mask=topo.mask(root, others[0]),
+                remote_sem=T.sem.arrived,
+                srcs=[T.land[:]],
+                dsts=[T.land[:] for c in others],
+                alu_op=0,
+            )],
+            local_sem=T.sem.read,
+        )
+        g.dma_start(T.y[:], T.land[:]).then_inc(T.sem.stored, 16)
+        g.wait_ge(T.sem.read, ENGINES)
+        g.wait_ge(T.sem.stored, 16)
+    else:
+        g.wait_ge(T.sem.arrived, ENGINES)
+        g.dma_start(T.y[:], T.land[:]).then_inc(T.sem.stored, 16)
+        g.wait_ge(T.sem.stored, 16)

@@ -1,42 +1,92 @@
 import concourse.bass as bass
 
+COLS = 512
 SCRATCH = {
-    "land": ("sbuf", [128, 512], "float32"),
+    "land": ("sbuf", [128, COLS], "float32"),
 }
-SEMAPHORES = ["loaded", "read", "arrived", "stored"]
+SEMAPHORES = ["loaded", "read", "seed", "arrived", "stored"]
 
-ENGINES = 16
+UNIT = 16
+
+
+def plan(cores, root, topo):
+    far = [c for c in cores if topo.die(c) != topo.die(root)]
+    near = [c for c in cores if topo.die(c) == topo.die(root) and c != root]
+    blocks = []
+    for group in (far, near):
+        units = COLS // UNIT
+        col = 0
+        for i, c in enumerate(group):
+            n = units // len(group) + (1 if i < units % len(group) else 0)
+            blocks.append((c, col, col + n * UNIT, [m for m in group if m != c]))
+            col += n * UNIT
+    calls = []
+    info = {}
+    widths = []
+    for b in blocks:
+        key = (b[2] - b[1], topo.die(b[0]))
+        if key not in widths:
+            widths.append(key)
+    for key in widths:
+        same = [b for b in blocks if (b[2] - b[1], topo.die(b[0])) == key]
+        engines = 16
+        while engines * len(same) > 16:
+            engines //= 2
+        call = []
+        for i, b in enumerate(same):
+            call.append((b[0], b[1], b[2], ((1 << engines) - 1) << (i * engines)))
+            info[b[0]] = (b[3], b[1], b[2], engines)
+        calls.append(call)
+    return calls, info
+
+
+def dst_id(topo, c):
+    a = topo.addr(c)
+    return bass.DstId(rid=a[0], pnc=a[1])
 
 
 def rank_program(g, core, T, topo):
-    rank = T.rank_of(core)
-    if rank is None:
+    if T.rank_of(core) is None:
         return
-    root = T.cores[0]
+    root = T.cores[T.root if T.root is not None else 0]
+    calls, info = plan(T.cores, root, topo)
 
     if core == root:
         g.dma_start(T.land[:], T.x[:]).then_inc(T.sem.loaded, 16)
         g.wait_ge(T.sem.loaded, 16)
-        others = [c for c in T.cores if c != root]
-        ids = []
-        for c in others:
-            a = topo.addr(c)
-            ids.append(bass.DstId(rid=a[0], pnc=a[1]))
-        g.remote_dma_fused(
-            [bass.RemoteDMATransfer(
-                dst_ids=ids,
-                dma_engine_mask=topo.mask(root, others[0]),
-                remote_sem=T.sem.arrived,
-                srcs=[T.land[:]],
-                dsts=[T.land[:] for c in others],
-                alu_op=0,
-            )],
-            local_sem=T.sem.read,
-        )
+        left = 0
+        for call in calls:
+            g.remote_dma_fused(
+                [bass.RemoteDMATransfer(
+                    dst_ids=[dst_id(topo, c)],
+                    dma_engine_mask=m,
+                    remote_sem=T.sem.seed,
+                    srcs=[T.land[:, a:b]],
+                    dsts=[T.land[:, a:b]],
+                    alu_op=0,
+                ) for (c, a, b, m) in call],
+                local_sem=T.sem.read,
+            )
+            left += sum(info[c][3] for (c, a, b, m) in call)
         g.dma_start(T.y[:], T.land[:]).then_inc(T.sem.stored, 16)
-        g.wait_ge(T.sem.read, ENGINES)
+        g.wait_ge(T.sem.read, left)
         g.wait_ge(T.sem.stored, 16)
-    else:
-        g.wait_ge(T.sem.arrived, ENGINES)
-        g.dma_start(T.y[:], T.land[:]).then_inc(T.sem.stored, 16)
-        g.wait_ge(T.sem.stored, 16)
+        return
+
+    mates, a, b, engines = info[core]
+    g.wait_ge(T.sem.seed, engines)
+    g.remote_dma_fused(
+        [bass.RemoteDMATransfer(
+            dst_ids=[dst_id(topo, m) for m in mates],
+            dma_engine_mask=topo.mask(core, mates[0]),
+            remote_sem=T.sem.arrived,
+            srcs=[T.land[:, a:b]],
+            dsts=[T.land[:, a:b] for m in mates],
+            alu_op=0,
+        )],
+        local_sem=T.sem.read,
+    )
+    g.wait_ge(T.sem.arrived, 16 * len(mates))
+    g.dma_start(T.y[:], T.land[:]).then_inc(T.sem.stored, 16)
+    g.wait_ge(T.sem.read, 16)
+    g.wait_ge(T.sem.stored, 16)

import concourse.bass as bass

COLS = 512
SCRATCH = {
    "land": ("sbuf", [128, COLS], "float32"),
}
SEMAPHORES = ["loaded", "read", "seed", "arrived", "stored"]

UNIT = 16


def plan(cores, root, topo):
    far = [c for c in cores if topo.die(c) != topo.die(root)]
    near = [c for c in cores if topo.die(c) == topo.die(root) and c != root]
    blocks = []
    for group in (far, near):
        units = COLS // UNIT
        col = 0
        for i, c in enumerate(group):
            n = units // len(group) + (1 if i < units % len(group) else 0)
            blocks.append((c, col, col + n * UNIT, [m for m in group if m != c]))
            col += n * UNIT
    calls = []
    info = {}
    widths = []
    for b in blocks:
        key = (b[2] - b[1], topo.die(b[0]))
        if key not in widths:
            widths.append(key)
    for key in widths:
        same = [b for b in blocks if (b[2] - b[1], topo.die(b[0])) == key]
        engines = 16
        while engines * len(same) > 16:
            engines //= 2
        call = []
        for i, b in enumerate(same):
            call.append((b[0], b[1], b[2], ((1 << engines) - 1) << (i * engines)))
            info[b[0]] = (b[3], b[1], b[2], engines)
        calls.append(call)
    return calls, info


def dst_id(topo, c):
    a = topo.addr(c)
    return bass.DstId(rid=a[0], pnc=a[1])


def rank_program(g, core, T, topo):
    if T.rank_of(core) is None:
        return
    root = T.cores[T.root if T.root is not None else 0]
    calls, info = plan(T.cores, root, topo)

    if core == root:
        g.dma_start(T.land[:], T.x[:]).then_inc(T.sem.loaded, 16)
        g.wait_ge(T.sem.loaded, 16)
        left = 0
        for call in calls:
            g.remote_dma_fused(
                [bass.RemoteDMATransfer(
                    dst_ids=[dst_id(topo, c)],
                    dma_engine_mask=m,
                    remote_sem=T.sem.seed,
                    srcs=[T.land[:, a:b]],
                    dsts=[T.land[:, a:b]],
                    alu_op=0,
                ) for (c, a, b, m) in call],
                local_sem=T.sem.read,
            )
            left += sum(info[c][3] for (c, a, b, m) in call)
        g.dma_start(T.y[:], T.land[:]).then_inc(T.sem.stored, 16)
        g.wait_ge(T.sem.read, left)
        g.wait_ge(T.sem.stored, 16)
        return

    mates, a, b, engines = info[core]
    g.wait_ge(T.sem.seed, engines)
    g.remote_dma_fused(
        [bass.RemoteDMATransfer(
            dst_ids=[dst_id(topo, m) for m in mates],
            dma_engine_mask=topo.mask(core, mates[0]),
            remote_sem=T.sem.arrived,
            srcs=[T.land[:, a:b]],
            dsts=[T.land[:, a:b] for m in mates],
            alu_op=0,
        )],
        local_sem=T.sem.read,
    )
    g.wait_ge(T.sem.arrived, 16 * len(mates))
    g.dma_start(T.y[:], T.land[:]).then_inc(T.sem.stored, 16)
    g.wait_ge(T.sem.read, 16)
    g.wait_ge(T.sem.stored, 16)
